import numpy as np
import ml_dtypes


def mxq(x, axis, fmt="e4m3"):
    dtype, down = {"e4m3": (ml_dtypes.float8_e4m3fn, 7), "e5m2": (ml_dtypes.float8_e5m2, 14)}[fmt]
    v = np.moveaxis(np.asarray(x, np.float32).astype(ml_dtypes.bfloat16).astype(np.float64), axis, -1)
    blocks = v.reshape(v.shape[:-1] + (-1, 32))
    amax = np.abs(blocks).max(-1, keepdims=True)
    byte = np.maximum(np.where(amax > 0, np.frexp(amax)[1] - 1 + 127, 0) - down, 1)
    scale = np.exp2(byte - 127.0)
    codes = (blocks / scale).astype(np.float32).astype(dtype).astype(np.float64)
    return np.moveaxis((codes * scale).reshape(v.shape), -1, axis)


WIDE = False


def mx_kscale(k):
    if not WIDE:
        return np.ones(k)
    levels = np.array([10, -10, 5, -5, 0])
    if k % 512:
        return np.exp2(np.random.permutation(np.resize(levels, k // 32))).repeat(32)
    a = np.empty((k // 512, 16))
    for p in range(k // 512):
        a[p, :8] = np.random.permutation(np.resize(levels, 8))
        for g in range(8):
            far = levels[np.abs(levels - a[p, g]) >= 10]
            a[p, g + 8] = far[np.random.randint(len(far))]
    return np.exp2(a.ravel()).repeat(32)


def f64(x):
    return np.asarray(x).astype(np.float64)


def striped(idx):
    return np.tile(idx.reshape(-1, 16).T, (8, 1)).astype(np.uint16)


def unstriped(offs):
    return offs[:16].T.reshape(-1).astype(np.int64)


def pack_weight(w):
    k, n = w.shape
    w = f64(np.asarray(w, np.float32).astype(ml_dtypes.bfloat16)).reshape(k // 32, 32, n)
    amax = np.abs(w).max(1)
    byte = np.clip(np.where(amax > 0, np.frexp(amax)[1] - 1 + 127 - 7, 1), 1, 254)
    scaled = (w * np.exp2(127.0 - byte)[:, None, :]).reshape(k, n).astype(np.float32)
    words = np.ascontiguousarray(scaled.reshape(k // 512, 128, 4, n).transpose(0, 1, 3, 2)).astype(ml_dtypes.float8_e4m3fn).view(np.uint8)
    return words, np.ascontiguousarray(byte.astype(np.uint8).reshape(k // 512, 16, n))


def unpack_weight(words, scales):
    g, p, n, _ = words.shape
    vals = np.ascontiguousarray(words).view(ml_dtypes.float8_e4m3fn).astype(np.float64) * np.repeat(np.exp2(scales.astype(np.float64) - 127.0), 8, axis=1)[..., None]
    return vals.transpose(0, 1, 3, 2).reshape(g * 512, n)

def planes(y):
    n, m = y.shape
    v = y.astype(np.float32).astype(ml_dtypes.bfloat16).astype(np.float64).reshape(n // 32, 32, m)
    top = np.abs(v).max(1)
    byte = np.clip(np.where(top > 0, np.frexp(top)[1] - 1 + 127 - 7, 1), 1, 254)
    codes = (v * np.exp2(127.0 - byte)[:, None, :]).reshape(n, m).astype(np.float32).astype(ml_dtypes.float8_e4m3fn).view(np.uint8)
    words = codes.reshape(n // 512, 128, 4, m).transpose(0, 1, 3, 2)
    return np.ascontiguousarray(words), np.ascontiguousarray(byte.astype(np.uint8).reshape(n // 512, 16, m))


K, T, S, N = 512, 1024, 512, 512


def setup_inputs():
    n = np.random.standard_normal
    s = mx_kscale(K)[:, None]
    packed_xT = pack_weight(n((K, T)) * s)
    return {
        "x_words": packed_xT[0],
        "x_scales": packed_xT[1],
        "w1": (n((K, N)) / np.sqrt(K) / s).astype(np.float32),
        "offs": striped(np.random.permutation(T)[:S]),
    }


def reference(x_words, x_scales, w1, offs):
    xq = unpack_weight(x_words, x_scales)[:, unstriped(offs)]
    y = mxq(f64(w1), 0, "e4m3").T @ xq
    e = np.exp(y - y.max(axis=1, keepdims=True))
    out_0 = e / e.sum(axis=1, keepdims=True)
    return (out_0,) + planes(out_0)

@@ -1,0 +1,103 @@
+from contextlib import ExitStack
+
+import concourse.mybir as mybir
+
+K, T, S, N = 512, 1024, 512, 512
+FLOPS = 2 * K * S * N
+BYTES = 4 * K * N + K * S + K * S // 32 + 128 * S // 16 * 2 + 4 * N * S + N * S + N * S // 32
+
+F32 = mybir.dt.float32
+BF16 = mybir.dt.bfloat16
+I32 = mybir.dt.int32
+U32 = mybir.dt.uint32
+U16 = mybir.dt.uint16
+U8 = mybir.dt.uint8
+FP8X4 = mybir.dt.float8_e4m3fn_x4
+ACT = mybir.ActivationFunctionType
+ALU = mybir.AluOpType
+AX = mybir.AxisListType
+
+P = 128
+PACK = 4
+
+
+def tile_picked_rank_none_po_kernel(tc, x_words, x_scales, w1, offs, out_0, out_1, out_2):
+    nc = tc.nc
+    with ExitStack() as ctx:
+        keep = ctx.enter_context(tc.tile_pool(name="keep", bufs=1))
+        psum = ctx.enter_context(tc.psum_pool(name="psum", bufs=1))
+
+        offsets = keep.tile([P, S // 16], U16, name="offsets")
+        nc.sync.dma_start(offsets[:], offs)
+
+        xs_all = keep.tile([P, T], U8, name="xs_all", align_bytes=64)
+        xs_rows = keep.tile([P, T], U8, name="xs_rows", align_bytes=64)
+        nc.vector.memset(xs_all[:].bitcast(I32), 0)
+        for q in range(4):
+            live = slice(32 * q, 32 * q + 4)
+            nc.sync.dma_start(xs_rows[live, :].bitcast(I32), x_scales[0][4 * q : 4 * q + 4, :].bitcast(I32))
+            nc.vector.tensor_copy(xs_all[live, :].bitcast(I32), xs_rows[live, :].bitcast(I32))
+
+        w_rows = w1.rearrange("(p j) c -> p j c", j=PACK)
+        w_lo = keep.tile([P, 2, N], F32, name="w_lo")
+        w_hi = keep.tile([P, 2, N], F32, name="w_hi")
+        xw_all = keep.tile([P, T], U32, name="xw_all", align_bytes=64)
+        nc.sync.dma_start(w_lo[:], w_rows[:, 0:2, :])
+        nc.sync.dma_start(xw_all[:].bitcast(I32), x_words[0].rearrange("p n t -> p (n t)").bitcast(I32))
+        nc.sync.dma_start(w_hi[:], w_rows[:, 2:4, :])
+
+        xs = keep.tile([P, S], U8, name="xs", align_bytes=64)
+        xw = keep.tile([P, S], U32, name="xw", align_bytes=64)
+        nc.vector.tensor_copy(xs[:], xs_all[:].indirect(offsets[:]))
+        nc.vector.tensor_copy(xw[:], xw_all[:].indirect(offsets[:]))
+
+        wb = keep.tile([P, PACK, P, PACK], BF16, name="wb", align_bytes=64)
+        wb_walk = wb[:].rearrange("p t m j -> p m t j")
+        lo_walk = w_lo[:].rearrange("p j (m t) -> p m t j", t=PACK)
+        hi_walk = w_hi[:].rearrange("p j (m t) -> p m t j", t=PACK)
+        nc.scalar.copy(wb_walk[:, :, :, 0:2], lo_walk)
+        split = 88
+        nc.vector.tensor_copy(wb_walk[:, :split, :, 2:4], hi_walk[:, :split])
+        nc.scalar.copy(wb_walk[:, split:, :, 2:4], hi_walk[:, split:])
+
+        wq = keep.tile([P, PACK, P], U32, name="wq", align_bytes=64)
+        ws = keep.tile([P, PACK, P], U8, name="ws", align_bytes=64)
+        banks = [psum.tile([P, S], F32, name=f"bank{t}") for t in range(PACK)]
+        for t in range(PACK):
+            nc.vector.quantize_mx(out=wq[:, t, :].bitcast(FP8X4), scales=ws[:, t, :], in_=wb[:, t].rearrange("p m j -> p (m j)"))
+            nc.tensor.matmul_mx(out=banks[t][:], lhsT=wq[:, t, :].bitcast(FP8X4), lhsT_scale=ws[:, t, :],
+                                rhs=xw[:].bitcast(FP8X4), rhs_scale=xs[:], start=True, stop=True)
+
+        neg_max = [keep.tile([P, 1], F32, name=f"neg_max{t}") for t in range(PACK)]
+        total = [keep.tile([P, 1], F32, name=f"total{t}") for t in range(PACK)]
+        inv = [keep.tile([P, 1], F32, name=f"inv{t}") for t in range(PACK)]
+        e = [keep.tile([P, S], F32, name=f"e{t}") for t in range(PACK)]
+        y = keep.tile([P, PACK, S], F32, name="y")
+        out_rows = out_0.rearrange("(p t) c -> p t c", t=PACK)
+        for t in range(PACK):
+            nc.vector.tensor_reduce(neg_max[t][:], banks[t][:], AX.X, ALU.max, negate=True)
+            nc.scalar.activation(e[t][:], banks[t][:], ACT.Exp, bias=neg_max[t][:], scale=1.0, accum_out=total[t][:])
+        for t in range(PACK):
+            nc.vector.reciprocal(inv[t][:], total[t][:])
+            nc.vector.tensor_scalar(y[:, t, :], e[t][:], inv[t][:], None, ALU.mult)
+            nc.sync.dma_start(out_rows[:, t, :], y[:, t, :])
+
+        yb = [keep.tile([P, S // 2, PACK], BF16, name=f"yb{h}", align_bytes=64) for h in range(2)]
+        yq = [keep.tile([P, S // 2], U32, name=f"yq{h}", align_bytes=64) for h in range(2)]
+        ys = keep.tile([P, S], U8, name="ys", align_bytes=64)
+
+        def weave(engine_copy, h, a, b):
+            engine_copy(yb[h][:, a:b, :].rearrange("p (c i) t -> p c t i", i=4),
+                        y[:, :, 256 * h + a : 256 * h + b].rearrange("p t (c i) -> p c t i", i=4))
+
+        weave(nc.vector.tensor_copy, 0, 0, 256)
+        weave(nc.scalar.copy, 1, 0, 128)
+        weave(nc.vector.tensor_copy, 1, 128, 256)
+        words_out = out_1[0].rearrange("p n t -> p (n t)").bitcast(I32)
+        for h in range(2):
+            cols = slice(256 * h, 256 * h + 256)
+            nc.vector.quantize_mx(out=yq[h][:].bitcast(FP8X4), scales=ys[:, cols], in_=yb[h][:].rearrange("p c t -> p (c t)"))
+            nc.sync.dma_start(words_out[:, cols], yq[h][:].bitcast(I32))
+        for q in range(4):
+            queue = nc.scalar if q % 2 == 0 else nc.sync
+            queue.dma_start(out_2[0][4 * q : 4 * q + 4, :].bitcast(I32), ys[32 * q : 32 * q + 4, :].bitcast(I32))

@@ -31,12 +31,9 @@ def tile_picked_rank_none_po_kernel(tc, x_words, x_scales, w1, offs, out_0, out_
         nc.sync.dma_start(offsets[:], offs)
 
         xs_all = keep.tile([P, T], U8, name="xs_all", align_bytes=64)
-        xs_rows = keep.tile([P, T], U8, name="xs_rows", align_bytes=64)
         nc.vector.memset(xs_all[:].bitcast(I32), 0)
         for q in range(4):
-            live = slice(32 * q, 32 * q + 4)
-            nc.sync.dma_start(xs_rows[live, :].bitcast(I32), x_scales[0][4 * q : 4 * q + 4, :].bitcast(I32))
-            nc.vector.tensor_copy(xs_all[live, :].bitcast(I32), xs_rows[live, :].bitcast(I32))
+            nc.scalar.dma_start(xs_all[32 * q : 32 * q + 4, :].bitcast(I32), x_scales[0][4 * q : 4 * q + 4, :].bitcast(I32))
 
         w_rows = w1.rearrange("(p j) c -> p j c", j=PACK)
         w_lo = keep.tile([P, 2, N], F32, name="w_lo")
@@ -51,20 +48,24 @@ def tile_picked_rank_none_po_kernel(tc, x_words, x_scales, w1, offs, out_0, out_
         nc.vector.tensor_copy(xs[:], xs_all[:].indirect(offsets[:]))
         nc.vector.tensor_copy(xw[:], xw_all[:].indirect(offsets[:]))
 
-        wb = keep.tile([P, PACK, P, PACK], BF16, name="wb", align_bytes=64)
-        wb_walk = wb[:].rearrange("p t m j -> p m t j")
-        lo_walk = w_lo[:].rearrange("p j (m t) -> p m t j", t=PACK)
-        hi_walk = w_hi[:].rearrange("p j (m t) -> p m t j", t=PACK)
-        nc.scalar.copy(wb_walk[:, :, :, 0:2], lo_walk)
-        split = 88
-        nc.vector.tensor_copy(wb_walk[:, :split, :, 2:4], hi_walk[:, :split])
-        nc.scalar.copy(wb_walk[:, split:, :, 2:4], hi_walk[:, split:])
+        wb = [keep.tile([P, 2, P, PACK], BF16, name=f"wb{u}", align_bytes=64) for u in range(2)]
+
+        def deal(engine_copy, src, j0, t0, t1):
+            u = t0 // 2
+            dst = wb[u][:, t0 - 2 * u : t1 - 2 * u, :, j0 : j0 + 2].rearrange("p t (a b) j -> p a t b j", b=2)
+            engine_copy(dst, src[:].rearrange("p j (a b t) -> p a t b j", b=2, t=PACK)[:, :, t0:t1])
+
+        deal(nc.scalar.copy, w_lo, 0, 0, 2)
+        deal(nc.scalar.copy, w_lo, 0, 2, 4)
+        deal(nc.vector.tensor_copy, w_hi, 2, 0, 1)
+        deal(nc.vector.tensor_copy, w_hi, 2, 1, 2)
+        deal(nc.scalar.copy, w_hi, 2, 2, 4)
 
         wq = keep.tile([P, PACK, P], U32, name="wq", align_bytes=64)
         ws = keep.tile([P, PACK, P], U8, name="ws", align_bytes=64)
         banks = [psum.tile([P, S], F32, name=f"bank{t}") for t in range(PACK)]
         for t in range(PACK):
-            nc.vector.quantize_mx(out=wq[:, t, :].bitcast(FP8X4), scales=ws[:, t, :], in_=wb[:, t].rearrange("p m j -> p (m j)"))
+            nc.vector.quantize_mx(out=wq[:, t, :].bitcast(FP8X4), scales=ws[:, t, :], in_=wb[t // 2][:, t % 2].rearrange("p m j -> p (m j)"))
             nc.tensor.matmul_mx(out=banks[t][:], lhsT=wq[:, t, :].bitcast(FP8X4), lhsT_scale=ws[:, t, :],
                                 rhs=xw[:].bitcast(FP8X4), rhs_scale=xs[:], start=True, stop=True)
 
@@ -74,13 +75,25 @@ def tile_picked_rank_none_po_kernel(tc, x_words, x_scales, w1, offs, out_0, out_
         e = [keep.tile([P, S], F32, name=f"e{t}") for t in range(PACK)]
         y = keep.tile([P, PACK, S], F32, name="y")
         out_rows = out_0.rearrange("(p t) c -> p t c", t=PACK)
-        for t in range(PACK):
+
+        def exponentials(t):
             nc.vector.tensor_reduce(neg_max[t][:], banks[t][:], AX.X, ALU.max, negate=True)
             nc.scalar.activation(e[t][:], banks[t][:], ACT.Exp, bias=neg_max[t][:], scale=1.0, accum_out=total[t][:])
-        for t in range(PACK):
-            nc.vector.reciprocal(inv[t][:], total[t][:])
-            nc.vector.tensor_scalar(y[:, t, :], e[t][:], inv[t][:], None, ALU.mult)
+
+        def normalise(t, cols):
+            nc.vector.tensor_scalar(y[:, t, cols], e[t][:, cols], inv[t][:], None, ALU.mult)
+
+        for t in range(3):
+            exponentials(t)
+        nc.vector.reciprocal(inv[0][:], total[0][:])
+        exponentials(3)
+        for t in range(3):
+            nc.vector.reciprocal(inv[t + 1][:], total[t + 1][:])
+            normalise(t, slice(0, S))
             nc.sync.dma_start(out_rows[:, t, :], y[:, t, :])
+        normalise(3, slice(0, 256))
+        nc.scalar.activation(y[:, 3, 256:], e[3][:, 256:], ACT.Copy, scale=inv[3][:])
+        nc.sync.dma_start(out_rows[:, 3, :], y[:, 3, :])
 
         yb = [keep.tile([P, S // 2, PACK], BF16, name=f"yb{h}", align_bytes=64) for h in range(2)]
         yq = [keep.tile([P, S // 2], U32, name=f"yq{h}", align_bytes=64) for h in range(2)]
@@ -91,8 +104,8 @@ def tile_picked_rank_none_po_kernel(tc, x_words, x_scales, w1, offs, out_0, out_
                         y[:, :, 256 * h + a : 256 * h + b].rearrange("p t (c i) -> p c t i", i=4))
 
         weave(nc.vector.tensor_copy, 0, 0, 256)
-        weave(nc.scalar.copy, 1, 0, 128)
-        weave(nc.vector.tensor_copy, 1, 128, 256)
+        weave(nc.scalar.copy, 1, 0, 160)
+        weave(nc.vector.tensor_copy, 1, 160, 256)
         words_out = out_1[0].rearrange("p n t -> p (n t)").bitcast(I32)
         for h in range(2):
             cols = slice(256 * h, 256 * h + 256)

@@ -28,18 +28,17 @@ def tile_picked_rank_none_po_kernel(tc, x_words, x_scales, w1, offs, out_0, out_
         psum = ctx.enter_context(tc.psum_pool(name="psum", bufs=1))
 
         offsets = keep.tile([P, S // 16], U16, name="offsets")
-        nc.sync.dma_start(offsets[:], offs)
 
         xs_all = keep.tile([P, T], U8, name="xs_all", align_bytes=64)
-        nc.vector.memset(xs_all[:].bitcast(I32), 0)
-        for q in range(4):
-            nc.scalar.dma_start(xs_all[32 * q : 32 * q + 4, :].bitcast(I32), x_scales[0][4 * q : 4 * q + 4, :].bitcast(I32))
-
+        xw_all = keep.tile([P, T], U32, name="xw_all", align_bytes=64)
         w_rows = w1.rearrange("(p j) c -> p j c", j=PACK)
         w_lo = keep.tile([P, 2, N], F32, name="w_lo")
         w_hi = keep.tile([P, 2, N], F32, name="w_hi")
-        xw_all = keep.tile([P, T], U32, name="xw_all", align_bytes=64)
+        nc.vector.memset(xs_all[:].bitcast(I32), 0)
         nc.sync.dma_start(w_lo[:], w_rows[:, 0:2, :])
+        nc.sync.dma_start(offsets[:], offs)
+        for q in range(4):
+            nc.sync.dma_start(xs_all[32 * q : 32 * q + 4, :].bitcast(I32), x_scales[0][4 * q : 4 * q + 4, :].bitcast(I32))
         nc.sync.dma_start(xw_all[:].bitcast(I32), x_words[0].rearrange("p n t -> p (n t)").bitcast(I32))
         nc.sync.dma_start(w_hi[:], w_rows[:, 2:4, :])
 
@@ -48,7 +47,7 @@ def tile_picked_rank_none_po_kernel(tc, x_words, x_scales, w1, offs, out_0, out_
         nc.vector.tensor_copy(xs[:], xs_all[:].indirect(offsets[:]))
         nc.vector.tensor_copy(xw[:], xw_all[:].indirect(offsets[:]))
 
-        wb = [keep.tile([P, 2, P, PACK], BF16, name=f"wb{u}", align_bytes=64) for u in range(2)]
+        wb = [keep.tile([P, 2, P, PACK], BF16, name=f"wb{u}", tag=f"wb{u}", align_bytes=64) for u in range(2)]
 
         def deal(engine_copy, src, j0, t0, t1):
             u = t0 // 2
@@ -70,47 +69,50 @@ def tile_picked_rank_none_po_kernel(tc, x_words, x_scales, w1, offs, out_0, out_
                                 rhs=xw[:].bitcast(FP8X4), rhs_scale=xs[:], start=True, stop=True)
 
         neg_max = [keep.tile([P, 1], F32, name=f"neg_max{t}") for t in range(PACK)]
-        total = [keep.tile([P, 1], F32, name=f"total{t}") for t in range(PACK)]
-        inv = [keep.tile([P, 1], F32, name=f"inv{t}") for t in range(PACK)]
+        total = keep.tile([P, PACK], F32, name="total")
+        inv = keep.tile([P, PACK], F32, name="inv")
         e = [keep.tile([P, S], F32, name=f"e{t}") for t in range(PACK)]
         y = keep.tile([P, PACK, S], F32, name="y")
         out_rows = out_0.rearrange("(p t) c -> p t c", t=PACK)
 
-        def exponentials(t):
+        for t in range(PACK):
             nc.vector.tensor_reduce(neg_max[t][:], banks[t][:], AX.X, ALU.max, negate=True)
-            nc.scalar.activation(e[t][:], banks[t][:], ACT.Exp, bias=neg_max[t][:], scale=1.0, accum_out=total[t][:])
+            nc.scalar.activation(e[t][:], banks[t][:], ACT.Exp, bias=neg_max[t][:], scale=1.0, accum_out=total[:, t : t + 1])
 
-        def normalise(t, cols):
-            nc.vector.tensor_scalar(y[:, t, cols], e[t][:, cols], inv[t][:], None, ALU.mult)
+        def normalise_on_vector(t, cols):
+            nc.vector.tensor_scalar(y[:, t, cols], e[t][:, cols], inv[:, t : t + 1], None, ALU.mult)
 
-        for t in range(3):
-            exponentials(t)
-        nc.vector.reciprocal(inv[0][:], total[0][:])
-        exponentials(3)
-        for t in range(3):
-            nc.vector.reciprocal(inv[t + 1][:], total[t + 1][:])
-            normalise(t, slice(0, S))
-            nc.sync.dma_start(out_rows[:, t, :], y[:, t, :])
-        normalise(3, slice(0, 256))
-        nc.scalar.activation(y[:, 3, 256:], e[3][:, 256:], ACT.Copy, scale=inv[3][:])
-        nc.sync.dma_start(out_rows[:, 3, :], y[:, 3, :])
+        def normalise_on_scalar(t, cols):
+            nc.scalar.activation(y[:, t, cols], e[t][:, cols], ACT.Copy, scale=inv[:, t : t + 1])
 
-        yb = [keep.tile([P, S // 2, PACK], BF16, name=f"yb{h}", align_bytes=64) for h in range(2)]
-        yq = [keep.tile([P, S // 2], U32, name=f"yq{h}", align_bytes=64) for h in range(2)]
+        nc.vector.reciprocal(inv[:, 0:2], total[:, 0:2])
+        normalise_on_vector(0, slice(0, S))
+        nc.sync.dma_start(out_rows[:, 0, :], y[:, 0, :])
+        nc.vector.reciprocal(inv[:, 2:3], total[:, 2:3])
+        normalise_on_vector(1, slice(0, S))
+        nc.sync.dma_start(out_rows[:, 1, :], y[:, 1, :])
+        normalise_on_scalar(2, slice(0, S))
+        nc.vector.reciprocal(inv[:, 3:4], total[:, 3:4])
+        normalise_on_vector(3, slice(0, S))
+        nc.sync.dma_start(out_rows[:, 2:4, :], y[:, 2:4, :])
+
+        pieces = [(0, 256), (256, 512)]
+        yb = [keep.tile([P, b - a, PACK], BF16, name=f"yb{h}", align_bytes=64) for h, (a, b) in enumerate(pieces)]
+        yq = [keep.tile([P, b - a], U32, name=f"yq{h}", align_bytes=64) for h, (a, b) in enumerate(pieces)]
         ys = keep.tile([P, S], U8, name="ys", align_bytes=64)
 
         def weave(engine_copy, h, a, b):
-            engine_copy(yb[h][:, a:b, :].rearrange("p (c i) t -> p c t i", i=4),
-                        y[:, :, 256 * h + a : 256 * h + b].rearrange("p t (c i) -> p c t i", i=4))
+            first = pieces[h][0]
+            engine_copy(yb[h][:, a - first : b - first, :].rearrange("p (c i) t -> p c t i", i=4),
+                        y[:, :, a:b].rearrange("p t (c i) -> p c t i", i=4))
 
         weave(nc.vector.tensor_copy, 0, 0, 256)
-        weave(nc.scalar.copy, 1, 0, 160)
-        weave(nc.vector.tensor_copy, 1, 160, 256)
+        weave(nc.scalar.copy, 1, 320, 512)
+        weave(nc.vector.tensor_copy, 1, 256, 320)
         words_out = out_1[0].rearrange("p n t -> p (n t)").bitcast(I32)
-        for h in range(2):
-            cols = slice(256 * h, 256 * h + 256)
-            nc.vector.quantize_mx(out=yq[h][:].bitcast(FP8X4), scales=ys[:, cols], in_=yb[h][:].rearrange("p c t -> p (c t)"))
-            nc.sync.dma_start(words_out[:, cols], yq[h][:].bitcast(I32))
+        for h, (a, b) in enumerate(pieces):
+            nc.vector.quantize_mx(out=yq[h][:].bitcast(FP8X4), scales=ys[:, a:b], in_=yb[h][:].rearrange("p c t -> p (c t)"))
+            nc.sync.dma_start(words_out[:, a:b], yq[h][:].bitcast(I32))
         for q in range(4):
             queue = nc.scalar if q % 2 == 0 else nc.sync
             queue.dma_start(out_2[0][4 * q : 4 * q + 4, :].bitcast(I32), ys[32 * q : 32 * q + 4, :].bitcast(I32))

@@ -76,6 +76,8 @@ def tile_picked_rank_none_po_kernel(tc, x_words, x_scales, w1, offs, out_0, out_
         out_rows = out_0.rearrange("(p t) c -> p t c", t=PACK)
 
         for t in range(PACK):
+            if t == PACK - 1:
+                nc.vector.reciprocal(inv[:, 0:1], total[:, 0:1])
             nc.vector.tensor_reduce(neg_max[t][:], banks[t][:], AX.X, ALU.max, negate=True)
             nc.scalar.activation(e[t][:], banks[t][:], ACT.Exp, bias=neg_max[t][:], scale=1.0, accum_out=total[:, t : t + 1])
 
@@ -85,7 +87,7 @@ def tile_picked_rank_none_po_kernel(tc, x_words, x_scales, w1, offs, out_0, out_
         def normalise_on_scalar(t, cols):
             nc.scalar.activation(y[:, t, cols], e[t][:, cols], ACT.Copy, scale=inv[:, t : t + 1])
 
-        nc.vector.reciprocal(inv[:, 0:2], total[:, 0:2])
+        nc.vector.reciprocal(inv[:, 1:2], total[:, 1:2])
         normalise_on_vector(0, slice(0, S))
         nc.sync.dma_start(out_rows[:, 0, :], y[:, 0, :])
         nc.vector.reciprocal(inv[:, 2:3], total[:, 2:3])
@@ -98,7 +100,7 @@ def tile_picked_rank_none_po_kernel(tc, x_words, x_scales, w1, offs, out_0, out_
 
         pieces = [(0, 256), (256, 512)]
         yb = [keep.tile([P, b - a, PACK], BF16, name=f"yb{h}", align_bytes=64) for h, (a, b) in enumerate(pieces)]
-        yq = [keep.tile([P, b - a], U32, name=f"yq{h}", align_bytes=64) for h, (a, b) in enumerate(pieces)]
+        yq = keep.tile([P, S], U32, name="yq", align_bytes=64)
         ys = keep.tile([P, S], U8, name="ys", align_bytes=64)
 
         def weave(engine_copy, h, a, b):
@@ -107,12 +109,12 @@ def tile_picked_rank_none_po_kernel(tc, x_words, x_scales, w1, offs, out_0, out_
                         y[:, :, a:b].rearrange("p t (c i) -> p c t i", i=4))
 
         weave(nc.vector.tensor_copy, 0, 0, 256)
-        weave(nc.scalar.copy, 1, 320, 512)
-        weave(nc.vector.tensor_copy, 1, 256, 320)
+        weave(nc.scalar.copy, 1, 336, 512)
+        weave(nc.vector.tensor_copy, 1, 256, 336)
         words_out = out_1[0].rearrange("p n t -> p (n t)").bitcast(I32)
         for h, (a, b) in enumerate(pieces):
-            nc.vector.quantize_mx(out=yq[h][:].bitcast(FP8X4), scales=ys[:, a:b], in_=yb[h][:].rearrange("p c t -> p (c t)"))
-            nc.sync.dma_start(words_out[:, a:b], yq[h][:].bitcast(I32))
+            nc.vector.quantize_mx(out=yq[:, a:b].bitcast(FP8X4), scales=ys[:, a:b], in_=yb[h][:].rearrange("p c t -> p (c t)"))
+        nc.sync.dma_start(words_out, yq[:].bitcast(I32))
         for q in range(4):
             queue = nc.scalar if q % 2 == 0 else nc.sync
             queue.dma_start(out_2[0][4 * q : 4 * q + 4, :].bitcast(I32), ys[32 * q : 32 * q + 4, :].bitcast(I32))

@@ -73,7 +73,8 @@ def tile_picked_rank_none_po_kernel(tc, x_words, x_scales, w1, offs, out_0, out_
         inv = keep.tile([P, PACK], F32, name="inv")
         e = [keep.tile([P, S], F32, name=f"e{t}") for t in range(PACK)]
         y = keep.tile([P, PACK, S], F32, name="y")
-        out_rows = out_0.rearrange("(p t) c -> p t c", t=PACK)
+        out_rows = out_0.rearrange("(p t) c -> p (t c)", t=PACK)
+        y_rows = y[:].rearrange("p t c -> p (t c)")
 
         for t in range(PACK):
             if t == PACK - 1:
@@ -89,14 +90,14 @@ def tile_picked_rank_none_po_kernel(tc, x_words, x_scales, w1, offs, out_0, out_
 
         nc.vector.reciprocal(inv[:, 1:2], total[:, 1:2])
         normalise_on_vector(0, slice(0, S))
-        nc.sync.dma_start(out_rows[:, 0, :], y[:, 0, :])
         nc.vector.reciprocal(inv[:, 2:3], total[:, 2:3])
-        normalise_on_vector(1, slice(0, S))
-        nc.sync.dma_start(out_rows[:, 1, :], y[:, 1, :])
+        normalise_on_vector(1, slice(0, 256))
+        nc.sync.dma_start(out_rows[:, :768], y_rows[:, :768])
         normalise_on_scalar(2, slice(0, S))
         nc.vector.reciprocal(inv[:, 3:4], total[:, 3:4])
+        normalise_on_vector(1, slice(256, S))
         normalise_on_vector(3, slice(0, S))
-        nc.sync.dma_start(out_rows[:, 2:4, :], y[:, 2:4, :])
+        nc.sync.dma_start(out_rows[:, 768:], y_rows[:, 768:])
 
         pieces = [(0, 256), (256, 512)]
         yb = [keep.tile([P, b - a, PACK], BF16, name=f"yb{h}", align_bytes=64) for h, (a, b) in enumerate(pieces)]
@@ -114,7 +115,7 @@ def tile_picked_rank_none_po_kernel(tc, x_words, x_scales, w1, offs, out_0, out_
         words_out = out_1[0].rearrange("p n t -> p (n t)").bitcast(I32)
         for h, (a, b) in enumerate(pieces):
             nc.vector.quantize_mx(out=yq[:, a:b].bitcast(FP8X4), scales=ys[:, a:b], in_=yb[h][:].rearrange("p c t -> p (c t)"))
-        nc.sync.dma_start(words_out, yq[:].bitcast(I32))
+            nc.sync.dma_start(words_out[:, a:b], yq[:, a:b].bitcast(I32))
         for q in range(4):
             queue = nc.scalar if q % 2 == 0 else nc.sync
             queue.dma_start(out_2[0][4 * q : 4 * q + 4, :].bitcast(I32), ys[32 * q : 32 * q + 4, :].bitcast(I32))

@@ -37,8 +37,8 @@ def tile_picked_rank_none_po_kernel(tc, x_words, x_scales, w1, offs, out_0, out_
         nc.vector.memset(xs_all[:].bitcast(I32), 0)
         nc.sync.dma_start(w_lo[:], w_rows[:, 0:2, :])
         nc.sync.dma_start(offsets[:], offs)
-        for q in range(4):
-            nc.sync.dma_start(xs_all[32 * q : 32 * q + 4, :].bitcast(I32), x_scales[0][4 * q : 4 * q + 4, :].bitcast(I32))
+        for r in range(4):
+            nc.sync.dma_start(xs_all[r:P:32, :].bitcast(I32), x_scales[0][r:16:4, :].bitcast(I32))
         nc.sync.dma_start(xw_all[:].bitcast(I32), x_words[0].rearrange("p n t -> p (n t)").bitcast(I32))
         nc.sync.dma_start(w_hi[:], w_rows[:, 2:4, :])
 
@@ -116,6 +116,6 @@ def tile_picked_rank_none_po_kernel(tc, x_words, x_scales, w1, offs, out_0, out_
         for h, (a, b) in enumerate(pieces):
             nc.vector.quantize_mx(out=yq[:, a:b].bitcast(FP8X4), scales=ys[:, a:b], in_=yb[h][:].rearrange("p c t -> p (c t)"))
             nc.sync.dma_start(words_out[:, a:b], yq[:, a:b].bitcast(I32))
-        for q in range(4):
-            queue = nc.scalar if q % 2 == 0 else nc.sync
-            queue.dma_start(out_2[0][4 * q : 4 * q + 4, :].bitcast(I32), ys[32 * q : 32 * q + 4, :].bitcast(I32))
+        for r in range(4):
+            queue = nc.scalar if r % 2 == 0 else nc.sync
+            queue.dma_start(out_2[0][r:16:4, :].bitcast(I32), ys[r:P:32, :].bitcast(I32))

@@ -47,25 +47,27 @@ def tile_picked_rank_none_po_kernel(tc, x_words, x_scales, w1, offs, out_0, out_
         nc.vector.tensor_copy(xs[:], xs_all[:].indirect(offsets[:]))
         nc.vector.tensor_copy(xw[:], xw_all[:].indirect(offsets[:]))
 
-        wb = [keep.tile([P, 2, P, PACK], BF16, name=f"wb{u}", tag=f"wb{u}", align_bytes=64) for u in range(2)]
+        groups = [(0, 1), (1, 2), (2, 4)]
+        wb = [keep.tile([P, t1 - t0, P, PACK], BF16, name=f"wb{t0}", tag=f"wb{t0}", align_bytes=64) for t0, t1 in groups]
 
-        def deal(engine_copy, src, j0, t0, t1):
-            u = t0 // 2
-            dst = wb[u][:, t0 - 2 * u : t1 - 2 * u, :, j0 : j0 + 2].rearrange("p t (a b) j -> p a t b j", b=2)
+        def deal(engine_copy, src, j0, u):
+            t0, t1 = groups[u]
+            dst = wb[u][:, :, :, j0 : j0 + 2].rearrange("p t (a b) j -> p a t b j", b=2)
             engine_copy(dst, src[:].rearrange("p j (a b t) -> p a t b j", b=2, t=PACK)[:, :, t0:t1])
 
-        deal(nc.scalar.copy, w_lo, 0, 0, 2)
-        deal(nc.scalar.copy, w_lo, 0, 2, 4)
-        deal(nc.vector.tensor_copy, w_hi, 2, 0, 1)
-        deal(nc.vector.tensor_copy, w_hi, 2, 1, 2)
-        deal(nc.scalar.copy, w_hi, 2, 2, 4)
+        for u in range(len(groups)):
+            deal(nc.scalar.copy, w_lo, 0, u)
+        deal(nc.scalar.copy, w_hi, 2, 0)
+        deal(nc.vector.tensor_copy, w_hi, 2, 1)
+        deal(nc.scalar.copy, w_hi, 2, 2)
+        rounded = [wb[0][:, 0], wb[1][:, 0], wb[2][:, 0], wb[2][:, 1]]
 
-        wq = keep.tile([P, PACK, P], U32, name="wq", align_bytes=64)
+        wq = [keep.tile([P, P], U32, name=f"wq{t}", tag="wb0" if t == 1 else f"wq{t}", align_bytes=64) for t in range(PACK)]
         ws = keep.tile([P, PACK, P], U8, name="ws", align_bytes=64)
         banks = [psum.tile([P, S], F32, name=f"bank{t}") for t in range(PACK)]
         for t in range(PACK):
-            nc.vector.quantize_mx(out=wq[:, t, :].bitcast(FP8X4), scales=ws[:, t, :], in_=wb[t // 2][:, t % 2].rearrange("p m j -> p (m j)"))
-            nc.tensor.matmul_mx(out=banks[t][:], lhsT=wq[:, t, :].bitcast(FP8X4), lhsT_scale=ws[:, t, :],
+            nc.vector.quantize_mx(out=wq[t][:].bitcast(FP8X4), scales=ws[:, t, :], in_=rounded[t].rearrange("p m j -> p (m j)"))
+            nc.tensor.matmul_mx(out=banks[t][:], lhsT=wq[t][:].bitcast(FP8X4), lhsT_scale=ws[:, t, :],
                                 rhs=xw[:].bitcast(FP8X4), rhs_scale=xs[:], start=True, stop=True)
 
         neg_max = [keep.tile([P, 1], F32, name=f"neg_max{t}") for t in range(PACK)]
@@ -91,13 +93,13 @@ def tile_picked_rank_none_po_kernel(tc, x_words, x_scales, w1, offs, out_0, out_
         nc.vector.reciprocal(inv[:, 1:2], total[:, 1:2])
         normalise_on_vector(0, slice(0, S))
         nc.vector.reciprocal(inv[:, 2:3], total[:, 2:3])
-        normalise_on_vector(1, slice(0, 256))
-        nc.sync.dma_start(out_rows[:, :768], y_rows[:, :768])
+        normalise_on_vector(1, slice(0, 384))
+        nc.sync.dma_start(out_rows[:, :896], y_rows[:, :896])
         normalise_on_scalar(2, slice(0, S))
         nc.vector.reciprocal(inv[:, 3:4], total[:, 3:4])
-        normalise_on_vector(1, slice(256, S))
+        normalise_on_vector(1, slice(384, S))
         normalise_on_vector(3, slice(0, S))
-        nc.sync.dma_start(out_rows[:, 768:], y_rows[:, 768:])
+        nc.sync.dma_start(out_rows[:, 896:], y_rows[:, 896:])
 
         pieces = [(0, 256), (256, 512)]
         yb = [keep.tile([P, b - a, PACK], BF16, name=f"yb{h}", align_bytes=64) for h, (a, b) in enumerate(pieces)]

@@ -19,6 +19,13 @@ AX = mybir.AxisListType
 
 P = 128
 PACK = 4
+QUADRANT = 32
+SCALE_ROWS = 16
+HALF = S // 2
+
+GROUPS = [(0, 1), (1, 2), (2, 4)]
+EARLY_COLUMNS = 384
+VECTOR_WEAVE = 336
 
 
 def tile_picked_rank_none_po_kernel(tc, x_words, x_scales, w1, offs, out_0, out_1, out_2):
@@ -37,8 +44,8 @@ def tile_picked_rank_none_po_kernel(tc, x_words, x_scales, w1, offs, out_0, out_
         nc.vector.memset(xs_all[:].bitcast(I32), 0)
         nc.sync.dma_start(w_lo[:], w_rows[:, 0:2, :])
         nc.sync.dma_start(offsets[:], offs)
-        for r in range(4):
-            nc.sync.dma_start(xs_all[r:P:32, :].bitcast(I32), x_scales[0][r:16:4, :].bitcast(I32))
+        for r in range(PACK):
+            nc.sync.dma_start(xs_all[r:P:QUADRANT, :].bitcast(I32), x_scales[0][r:SCALE_ROWS:PACK, :].bitcast(I32))
         nc.sync.dma_start(xw_all[:].bitcast(I32), x_words[0].rearrange("p n t -> p (n t)").bitcast(I32))
         nc.sync.dma_start(w_hi[:], w_rows[:, 2:4, :])
 
@@ -47,28 +54,28 @@ def tile_picked_rank_none_po_kernel(tc, x_words, x_scales, w1, offs, out_0, out_
         nc.vector.tensor_copy(xs[:], xs_all[:].indirect(offsets[:]))
         nc.vector.tensor_copy(xw[:], xw_all[:].indirect(offsets[:]))
 
-        groups = [(0, 1), (1, 2), (2, 4)]
-        wb = [keep.tile([P, t1 - t0, P, PACK], BF16, name=f"wb{t0}", tag=f"wb{t0}", align_bytes=64) for t0, t1 in groups]
+        wb = [keep.tile([P, t1 - t0, P, PACK], BF16, name=f"wb{t0}", tag=f"wb{t0}", align_bytes=64) for t0, t1 in GROUPS]
 
         def deal(engine_copy, src, j0, u):
-            t0, t1 = groups[u]
+            t0, t1 = GROUPS[u]
             dst = wb[u][:, :, :, j0 : j0 + 2].rearrange("p t (a b) j -> p a t b j", b=2)
             engine_copy(dst, src[:].rearrange("p j (a b t) -> p a t b j", b=2, t=PACK)[:, :, t0:t1])
 
-        for u in range(len(groups)):
+        for u in range(len(GROUPS)):
             deal(nc.scalar.copy, w_lo, 0, u)
         deal(nc.scalar.copy, w_hi, 2, 0)
         deal(nc.vector.tensor_copy, w_hi, 2, 1)
         deal(nc.scalar.copy, w_hi, 2, 2)
-        rounded = [wb[0][:, 0], wb[1][:, 0], wb[2][:, 0], wb[2][:, 1]]
 
-        wq = [keep.tile([P, P], U32, name=f"wq{t}", tag="wb0" if t == 1 else f"wq{t}", align_bytes=64) for t in range(PACK)]
+        wq = [keep.tile([P, t1 - t0, P], U32, name=f"wq{t0}", tag="wb0" if t0 == 1 else f"wq{t0}", align_bytes=64) for t0, t1 in GROUPS]
         ws = keep.tile([P, PACK, P], U8, name="ws", align_bytes=64)
         banks = [psum.tile([P, S], F32, name=f"bank{t}") for t in range(PACK)]
-        for t in range(PACK):
-            nc.vector.quantize_mx(out=wq[t][:].bitcast(FP8X4), scales=ws[:, t, :], in_=rounded[t].rearrange("p m j -> p (m j)"))
-            nc.tensor.matmul_mx(out=banks[t][:], lhsT=wq[t][:].bitcast(FP8X4), lhsT_scale=ws[:, t, :],
-                                rhs=xw[:].bitcast(FP8X4), rhs_scale=xs[:], start=True, stop=True)
+        for u, (t0, t1) in enumerate(GROUPS):
+            nc.vector.quantize_mx(out=wq[u][:].rearrange("p t m -> p (t m)").bitcast(FP8X4), scales=ws[:, t0:t1, :].rearrange("p t m -> p (t m)"),
+                                  in_=wb[u][:].rearrange("p t m j -> p (t m j)"))
+            for t in range(t0, t1):
+                nc.tensor.matmul_mx(out=banks[t][:], lhsT=wq[u][:, t - t0, :].bitcast(FP8X4), lhsT_scale=ws[:, t, :],
+                                    rhs=xw[:].bitcast(FP8X4), rhs_scale=xs[:], start=True, stop=True)
 
         neg_max = [keep.tile([P, 1], F32, name=f"neg_max{t}") for t in range(PACK)]
         total = keep.tile([P, PACK], F32, name="total")
@@ -78,11 +85,8 @@ def tile_picked_rank_none_po_kernel(tc, x_words, x_scales, w1, offs, out_0, out_
         out_rows = out_0.rearrange("(p t) c -> p (t c)", t=PACK)
         y_rows = y[:].rearrange("p t c -> p (t c)")
 
-        for t in range(PACK):
-            if t == PACK - 1:
-                nc.vector.reciprocal(inv[:, 0:1], total[:, 0:1])
-            nc.vector.tensor_reduce(neg_max[t][:], banks[t][:], AX.X, ALU.max, negate=True)
-            nc.scalar.activation(e[t][:], banks[t][:], ACT.Exp, bias=neg_max[t][:], scale=1.0, accum_out=total[:, t : t + 1])
+        def invert(t):
+            nc.vector.reciprocal(inv[:, t : t + 1], total[:, t : t + 1])
 
         def normalise_on_vector(t, cols):
             nc.vector.tensor_scalar(y[:, t, cols], e[t][:, cols], inv[:, t : t + 1], None, ALU.mult)
@@ -90,34 +94,44 @@ def tile_picked_rank_none_po_kernel(tc, x_words, x_scales, w1, offs, out_0, out_
         def normalise_on_scalar(t, cols):
             nc.scalar.activation(y[:, t, cols], e[t][:, cols], ACT.Copy, scale=inv[:, t : t + 1])
 
-        nc.vector.reciprocal(inv[:, 1:2], total[:, 1:2])
-        normalise_on_vector(0, slice(0, S))
-        nc.vector.reciprocal(inv[:, 2:3], total[:, 2:3])
-        normalise_on_vector(1, slice(0, 384))
-        nc.sync.dma_start(out_rows[:, :896], y_rows[:, :896])
-        normalise_on_scalar(2, slice(0, S))
-        nc.vector.reciprocal(inv[:, 3:4], total[:, 3:4])
-        normalise_on_vector(1, slice(384, S))
-        normalise_on_vector(3, slice(0, S))
-        nc.sync.dma_start(out_rows[:, 896:], y_rows[:, 896:])
+        for t in range(PACK):
+            if t == PACK - 1:
+                invert(0)
+            nc.vector.tensor_reduce(neg_max[t][:], banks[t][:], AX.X, ALU.max, negate=True)
+            nc.scalar.activation(e[t][:], banks[t][:], ACT.Exp, bias=neg_max[t][:], scale=1.0, accum_out=total[:, t : t + 1])
 
-        pieces = [(0, 256), (256, 512)]
-        yb = [keep.tile([P, b - a, PACK], BF16, name=f"yb{h}", align_bytes=64) for h, (a, b) in enumerate(pieces)]
+        first_store = S + EARLY_COLUMNS
+        invert(1)
+        normalise_on_vector(0, slice(0, S))
+        invert(2)
+        normalise_on_vector(1, slice(0, EARLY_COLUMNS))
+        nc.sync.dma_start(out_rows[:, :first_store], y_rows[:, :first_store])
+        normalise_on_scalar(2, slice(0, HALF))
+        normalise_on_scalar(2, slice(HALF, S))
+        invert(3)
+        normalise_on_vector(1, slice(EARLY_COLUMNS, S))
+        normalise_on_vector(3, slice(0, HALF))
+        normalise_on_vector(3, slice(HALF, S))
+        nc.sync.dma_start(out_rows[:, first_store:], y_rows[:, first_store:])
+
+        yb = [keep.tile([P, HALF, PACK], BF16, name=f"yb{h}", align_bytes=64) for h in range(2)]
         yq = keep.tile([P, S], U32, name="yq", align_bytes=64)
         ys = keep.tile([P, S], U8, name="ys", align_bytes=64)
 
-        def weave(engine_copy, h, a, b):
-            first = pieces[h][0]
-            engine_copy(yb[h][:, a - first : b - first, :].rearrange("p (c i) t -> p c t i", i=4),
+        def weave(engine_copy, a, b):
+            h = a // HALF
+            engine_copy(yb[h][:, a - HALF * h : b - HALF * h, :].rearrange("p (c i) t -> p c t i", i=4),
                         y[:, :, a:b].rearrange("p t (c i) -> p c t i", i=4))
 
-        weave(nc.vector.tensor_copy, 0, 0, 256)
-        weave(nc.scalar.copy, 1, 336, 512)
-        weave(nc.vector.tensor_copy, 1, 256, 336)
+        weave(nc.vector.tensor_copy, 0, HALF)
+        weave(nc.scalar.copy, VECTOR_WEAVE, S)
+        weave(nc.vector.tensor_copy, HALF, VECTOR_WEAVE)
+
         words_out = out_1[0].rearrange("p n t -> p (n t)").bitcast(I32)
-        for h, (a, b) in enumerate(pieces):
-            nc.vector.quantize_mx(out=yq[:, a:b].bitcast(FP8X4), scales=ys[:, a:b], in_=yb[h][:].rearrange("p c t -> p (c t)"))
-            nc.sync.dma_start(words_out[:, a:b], yq[:, a:b].bitcast(I32))
-        for r in range(4):
+        for h in range(2):
+            cols = slice(HALF * h, HALF * (h + 1))
+            nc.vector.quantize_mx(out=yq[:, cols].bitcast(FP8X4), scales=ys[:, cols], in_=yb[h][:].rearrange("p c t -> p (c t)"))
+            nc.sync.dma_start(words_out[:, cols], yq[:, cols].bitcast(I32))
+        for r in range(PACK):
             queue = nc.scalar if r % 2 == 0 else nc.sync
-            queue.dma_start(out_2[0][r:16:4, :].bitcast(I32), ys[r:P:32, :].bitcast(I32))
+            queue.dma_start(out_2[0][r:SCALE_ROWS:PACK, :].bitcast(I32), ys[r:P:QUADRANT, :].bitcast(I32))

@@ -22,6 +22,7 @@ PACK = 4
 QUADRANT = 32
 SCALE_ROWS = 16
 HALF = S // 2
+EARLY_M = 80
 
 GROUPS = [(0, 1), (1, 2), (2, 4)]
 EARLY_COLUMNS = 384
@@ -39,40 +40,37 @@ def tile_picked_rank_none_po_kernel(tc, x_words, x_scales, w1, offs, out_0, out_
         xs_all = keep.tile([P, T], U8, name="xs_all", align_bytes=64)
         xw_all = keep.tile([P, T], U32, name="xw_all", align_bytes=64)
         w_rows = w1.rearrange("(p j) c -> p j c", j=PACK)
-        w_lo = keep.tile([P, 2, N], F32, name="w_lo")
-        w_hi = keep.tile([P, 2, N], F32, name="w_hi")
+        w_lo = keep.tile([P, PACK, PACK * EARLY_M], F32, name="w_lo")
+        w_hi = keep.tile([P, PACK, N - PACK * EARLY_M], F32, name="w_hi")
         nc.vector.memset(xs_all[:].bitcast(I32), 0)
-        nc.sync.dma_start(w_lo[:], w_rows[:, 0:2, :])
+        nc.sync.dma_start(w_lo[:], w_rows[:, :, : PACK * EARLY_M])
         nc.sync.dma_start(offsets[:], offs)
         for r in range(PACK):
             nc.sync.dma_start(xs_all[r:P:QUADRANT, :].bitcast(I32), x_scales[0][r:SCALE_ROWS:PACK, :].bitcast(I32))
         nc.sync.dma_start(xw_all[:].bitcast(I32), x_words[0].rearrange("p n t -> p (n t)").bitcast(I32))
-        nc.sync.dma_start(w_hi[:], w_rows[:, 2:4, :])
+        nc.sync.dma_start(w_hi[:], w_rows[:, :, PACK * EARLY_M :])
 
         xs = keep.tile([P, S], U8, name="xs", align_bytes=64)
         xw = keep.tile([P, S], U32, name="xw", align_bytes=64)
         nc.vector.tensor_copy(xs[:], xs_all[:].indirect(offsets[:]))
         nc.vector.tensor_copy(xw[:], xw_all[:].indirect(offsets[:]))
 
-        wb = [keep.tile([P, t1 - t0, P, PACK], BF16, name=f"wb{t0}", tag=f"wb{t0}", align_bytes=64) for t0, t1 in GROUPS]
+        wb = [keep.tile([P, 2, P, PACK], BF16, name=f"wb{u}", align_bytes=64) for u in range(2)]
 
-        def deal(engine_copy, src, j0, u):
-            t0, t1 = GROUPS[u]
-            dst = wb[u][:, :, :, j0 : j0 + 2].rearrange("p t (a b) j -> p a t b j", b=2)
-            engine_copy(dst, src[:].rearrange("p j (a b t) -> p a t b j", b=2, t=PACK)[:, :, t0:t1])
+        def deal(src, m0, m1, t0, t1):
+            nc.scalar.copy(wb[t0 // 2][:, :, m0:m1, :].rearrange("p t m j -> p m j t"),
+                        src[:].rearrange("p j (m t) -> p m j t", t=PACK)[:, :, :, t0:t1])
 
-        for u in range(len(GROUPS)):
-            deal(nc.scalar.copy, w_lo, 0, u)
-        deal(nc.scalar.copy, w_hi, 2, 0)
-        deal(nc.vector.tensor_copy, w_hi, 2, 1)
-        deal(nc.scalar.copy, w_hi, 2, 2)
+        for src, m0, m1 in ((w_lo, 0, EARLY_M), (w_hi, EARLY_M, P)):
+            deal(src, m0, m1, 0, 2)
+            deal(src, m0, m1, 2, 4)
 
-        wq = [keep.tile([P, t1 - t0, P], U32, name=f"wq{t0}", tag="wb0" if t0 == 1 else f"wq{t0}", align_bytes=64) for t0, t1 in GROUPS]
+        wq = [keep.tile([P, t1 - t0, P], U32, name=f"wq{t0}", align_bytes=64) for t0, t1 in GROUPS]
         ws = keep.tile([P, PACK, P], U8, name="ws", align_bytes=64)
         banks = [psum.tile([P, S], F32, name=f"bank{t}") for t in range(PACK)]
         for u, (t0, t1) in enumerate(GROUPS):
             nc.vector.quantize_mx(out=wq[u][:].rearrange("p t m -> p (t m)").bitcast(FP8X4), scales=ws[:, t0:t1, :].rearrange("p t m -> p (t m)"),
-                                  in_=wb[u][:].rearrange("p t m j -> p (t m j)"))
+                                  in_=wb[t0 // 2][:, t0 % 2 : t0 % 2 + t1 - t0].rearrange("p t m j -> p (t m j)"))
             for t in range(t0, t1):
                 nc.tensor.matmul_mx(out=banks[t][:], lhsT=wq[u][:, t - t0, :].bitcast(FP8X4), lhsT_scale=ws[:, t, :],
                                     rhs=xw[:].bitcast(FP8X4), rhs_scale=xs[:], start=True, stop=True)

@@ -22,7 +22,8 @@ PACK = 4
 QUADRANT = 32
 SCALE_ROWS = 16
 HALF = S // 2
-EARLY_M = 80
+EARLY_M = 64
+SCALAR_M = 112
 
 GROUPS = [(0, 1), (1, 2), (2, 4)]
 EARLY_COLUMNS = 384
@@ -55,17 +56,19 @@ def tile_picked_rank_none_po_kernel(tc, x_words, x_scales, w1, offs, out_0, out_
         nc.vector.tensor_copy(xs[:], xs_all[:].indirect(offsets[:]))
         nc.vector.tensor_copy(xw[:], xw_all[:].indirect(offsets[:]))
 
-        wb = [keep.tile([P, 2, P, PACK], BF16, name=f"wb{u}", align_bytes=64) for u in range(2)]
+        wb = [keep.tile([P, 2, P, PACK], BF16, name=f"wb{u}", tag=f"wb{u}", align_bytes=64) for u in range(2)]
 
-        def deal(src, m0, m1, t0, t1):
-            nc.scalar.copy(wb[t0 // 2][:, :, m0:m1, :].rearrange("p t m j -> p m j t"),
-                        src[:].rearrange("p j (m t) -> p m j t", t=PACK)[:, :, :, t0:t1])
+        def deal(engine_copy, src, first_m, m0, m1, t0, t1):
+            engine_copy(wb[t0 // 2][:, :, m0:m1, :].rearrange("p t m j -> p m j t"),
+                        src[:].rearrange("p j (m t) -> p m j t", t=PACK)[:, m0 - first_m : m1 - first_m, :, t0:t1])
 
-        for src, m0, m1 in ((w_lo, 0, EARLY_M), (w_hi, EARLY_M, P)):
-            deal(src, m0, m1, 0, 2)
-            deal(src, m0, m1, 2, 4)
+        deal(nc.scalar.copy, w_lo, 0, 0, EARLY_M, 0, 2)
+        deal(nc.scalar.copy, w_lo, 0, 0, EARLY_M, 2, 4)
+        deal(nc.scalar.copy, w_hi, EARLY_M, EARLY_M, SCALAR_M, 0, 2)
+        deal(nc.vector.tensor_copy, w_hi, EARLY_M, SCALAR_M, P, 0, 2)
+        deal(nc.vector.tensor_copy, w_hi, EARLY_M, EARLY_M, P, 2, 4)
 
-        wq = [keep.tile([P, t1 - t0, P], U32, name=f"wq{t0}", align_bytes=64) for t0, t1 in GROUPS]
+        wq = [keep.tile([P, t1 - t0, P], U32, name=f"wq{t0}", tag="wb0" if t0 == 2 else f"wq{t0}", align_bytes=64) for t0, t1 in GROUPS]
         ws = keep.tile([P, PACK, P], U8, name="ws", align_bytes=64)
         banks = [psum.tile([P, S], F32, name=f"bank{t}") for t in range(PACK)]
         for u, (t0, t1) in enumerate(GROUPS):

@@ -22,8 +22,9 @@ PACK = 4
 QUADRANT = 32
 SCALE_ROWS = 16
 HALF = S // 2
-EARLY_M = 64
-SCALAR_M = 112
+EARLY_M = 96
+SCALAR_M = 72
+VECTOR_M = 64
 
 GROUPS = [(0, 1), (1, 2), (2, 4)]
 EARLY_COLUMNS = 384
@@ -44,17 +45,17 @@ def tile_picked_rank_none_po_kernel(tc, x_words, x_scales, w1, offs, out_0, out_
         w_lo = keep.tile([P, PACK, PACK * EARLY_M], F32, name="w_lo")
         w_hi = keep.tile([P, PACK, N - PACK * EARLY_M], F32, name="w_hi")
         nc.vector.memset(xs_all[:].bitcast(I32), 0)
-        nc.sync.dma_start(w_lo[:], w_rows[:, :, : PACK * EARLY_M])
+        nc.sync.dma_start(xw_all[:].bitcast(I32), x_words[0].rearrange("p n t -> p (n t)").bitcast(I32))
         nc.sync.dma_start(offsets[:], offs)
         for r in range(PACK):
             nc.sync.dma_start(xs_all[r:P:QUADRANT, :].bitcast(I32), x_scales[0][r:SCALE_ROWS:PACK, :].bitcast(I32))
-        nc.sync.dma_start(xw_all[:].bitcast(I32), x_words[0].rearrange("p n t -> p (n t)").bitcast(I32))
+        nc.sync.dma_start(w_lo[:], w_rows[:, :, : PACK * EARLY_M])
         nc.sync.dma_start(w_hi[:], w_rows[:, :, PACK * EARLY_M :])
 
         xs = keep.tile([P, S], U8, name="xs", align_bytes=64)
         xw = keep.tile([P, S], U32, name="xw", align_bytes=64)
-        nc.vector.tensor_copy(xs[:], xs_all[:].indirect(offsets[:]))
         nc.vector.tensor_copy(xw[:], xw_all[:].indirect(offsets[:]))
+        nc.vector.tensor_copy(xs[:], xs_all[:].indirect(offsets[:]))
 
         wb = [keep.tile([P, 2, P, PACK], BF16, name=f"wb{u}", tag=f"wb{u}", align_bytes=64) for u in range(2)]
 
@@ -62,11 +63,12 @@ def tile_picked_rank_none_po_kernel(tc, x_words, x_scales, w1, offs, out_0, out_
             engine_copy(wb[t0 // 2][:, :, m0:m1, :].rearrange("p t m j -> p m j t"),
                         src[:].rearrange("p j (m t) -> p m j t", t=PACK)[:, m0 - first_m : m1 - first_m, :, t0:t1])
 
-        deal(nc.scalar.copy, w_lo, 0, 0, EARLY_M, 0, 2)
-        deal(nc.scalar.copy, w_lo, 0, 0, EARLY_M, 2, 4)
-        deal(nc.scalar.copy, w_hi, EARLY_M, EARLY_M, SCALAR_M, 0, 2)
-        deal(nc.vector.tensor_copy, w_hi, EARLY_M, SCALAR_M, P, 0, 2)
-        deal(nc.vector.tensor_copy, w_hi, EARLY_M, EARLY_M, P, 2, 4)
+        deal(nc.scalar.copy, w_lo, 0, 0, SCALAR_M, 0, 2)
+        deal(nc.vector.tensor_copy, w_lo, 0, SCALAR_M, EARLY_M, 0, 2)
+        deal(nc.vector.tensor_copy, w_lo, 0, 0, VECTOR_M, 2, 4)
+        deal(nc.scalar.copy, w_hi, EARLY_M, EARLY_M, P, 0, 2)
+        deal(nc.scalar.copy, w_lo, 0, VECTOR_M, EARLY_M, 2, 4)
+        deal(nc.scalar.copy, w_hi, EARLY_M, EARLY_M, P, 2, 4)
 
         wq = [keep.tile([P, t1 - t0, P], U32, name=f"wq{t0}", tag="wb0" if t0 == 2 else f"wq{t0}", align_bytes=64) for t0, t1 in GROUPS]
         ws = keep.tile([P, PACK, P], U8, name="ws", align_bytes=64)

@@ -24,7 +24,7 @@ SCALE_ROWS = 16
 HALF = S // 2
 EARLY_M = 96
 SCALAR_M = 72
-VECTOR_M = 64
+VECTOR_M = 56
 
 GROUPS = [(0, 1), (1, 2), (2, 4)]
 EARLY_COLUMNS = 384
@@ -74,8 +74,9 @@ def tile_picked_rank_none_po_kernel(tc, x_words, x_scales, w1, offs, out_0, out_
         ws = keep.tile([P, PACK, P], U8, name="ws", align_bytes=64)
         banks = [psum.tile([P, S], F32, name=f"bank{t}") for t in range(PACK)]
         for u, (t0, t1) in enumerate(GROUPS):
-            nc.vector.quantize_mx(out=wq[u][:].rearrange("p t m -> p (t m)").bitcast(FP8X4), scales=ws[:, t0:t1, :].rearrange("p t m -> p (t m)"),
-                                  in_=wb[t0 // 2][:, t0 % 2 : t0 % 2 + t1 - t0].rearrange("p t m j -> p (t m j)"))
+            for cols in ((slice(0, P // 2), slice(P // 2, P)) if u == 0 else (slice(0, P),)):
+                nc.vector.quantize_mx(out=wq[u][:, :, cols].rearrange("p t m -> p (t m)").bitcast(FP8X4), scales=ws[:, t0:t1, cols].rearrange("p t m -> p (t m)"),
+                                      in_=wb[t0 // 2][:, t0 % 2 : t0 % 2 + t1 - t0, cols].rearrange("p t m j -> p (t m j)"))
             for t in range(t0, t1):
                 nc.tensor.matmul_mx(out=banks[t][:], lhsT=wq[u][:, t - t0, :].bitcast(FP8X4), lhsT_scale=ws[:, t, :],
                                     rhs=xw[:].bitcast(FP8X4), rhs_scale=xs[:], start=True, stop=True)

@@ -124,8 +124,8 @@ def tile_picked_rank_none_po_kernel(tc, x_words, x_scales, w1, offs, out_0, out_
 
         def weave(engine_copy, a, b):
             h = a // HALF
-            engine_copy(yb[h][:, a - HALF * h : b - HALF * h, :].rearrange("p (c i) t -> p c t i", i=4),
-                        y[:, :, a:b].rearrange("p t (c i) -> p c t i", i=4))
+            engine_copy(yb[h][:, a - HALF * h : b - HALF * h, :].rearrange("p (c i) t -> p c t i", i=2),
+                        y[:, :, a:b].rearrange("p t (c i) -> p c t i", i=2))
 
         weave(nc.vector.tensor_copy, 0, HALF)
         weave(nc.scalar.copy, VECTOR_WEAVE, S)

@@ -27,8 +27,9 @@ SCALAR_M = 72
 VECTOR_M = 56
 
 GROUPS = [(0, 1), (1, 2), (2, 4)]
+FIRST_TILE_PARTS = [slice(0, P // 2), slice(P // 2, P)]
 EARLY_COLUMNS = 384
-VECTOR_WEAVE = 336
+VECTOR_WEAVE = (176, 400)
 
 
 def tile_picked_rank_none_po_kernel(tc, x_words, x_scales, w1, offs, out_0, out_1, out_2):
@@ -57,26 +58,28 @@ def tile_picked_rank_none_po_kernel(tc, x_words, x_scales, w1, offs, out_0, out_
         nc.vector.tensor_copy(xw[:], xw_all[:].indirect(offsets[:]))
         nc.vector.tensor_copy(xs[:], xs_all[:].indirect(offsets[:]))
 
-        wb = [keep.tile([P, 2, P, PACK], BF16, name=f"wb{u}", tag=f"wb{u}", align_bytes=64) for u in range(2)]
+        wb = [keep.tile([P, 2, P, PACK], BF16, name=f"wb{pair}", tag=f"wb{pair}", align_bytes=64) for pair in range(2)]
 
-        def deal(engine_copy, src, first_m, m0, m1, t0, t1):
-            engine_copy(wb[t0 // 2][:, :, m0:m1, :].rearrange("p t m j -> p m j t"),
-                        src[:].rearrange("p j (m t) -> p m j t", t=PACK)[:, m0 - first_m : m1 - first_m, :, t0:t1])
+        def deal(engine_copy, pair, m0, m1):
+            src, first_m = (w_lo, 0) if m0 < EARLY_M else (w_hi, EARLY_M)
+            engine_copy(wb[pair][:, :, m0:m1, :].rearrange("p t m j -> p m j t"),
+                        src[:].rearrange("p j (m t) -> p m j t", t=PACK)[:, m0 - first_m : m1 - first_m, :, 2 * pair : 2 * pair + 2])
 
-        deal(nc.scalar.copy, w_lo, 0, 0, SCALAR_M, 0, 2)
-        deal(nc.vector.tensor_copy, w_lo, 0, SCALAR_M, EARLY_M, 0, 2)
-        deal(nc.vector.tensor_copy, w_lo, 0, 0, VECTOR_M, 2, 4)
-        deal(nc.scalar.copy, w_hi, EARLY_M, EARLY_M, P, 0, 2)
-        deal(nc.scalar.copy, w_lo, 0, VECTOR_M, EARLY_M, 2, 4)
-        deal(nc.scalar.copy, w_hi, EARLY_M, EARLY_M, P, 2, 4)
+        deal(nc.scalar.copy, 0, 0, SCALAR_M)
+        deal(nc.vector.tensor_copy, 0, SCALAR_M, EARLY_M)
+        deal(nc.vector.tensor_copy, 1, 0, VECTOR_M)
+        deal(nc.scalar.copy, 0, EARLY_M, P)
+        deal(nc.scalar.copy, 1, VECTOR_M, EARLY_M)
+        deal(nc.scalar.copy, 1, EARLY_M, P)
 
         wq = [keep.tile([P, t1 - t0, P], U32, name=f"wq{t0}", tag="wb0" if t0 == 2 else f"wq{t0}", align_bytes=64) for t0, t1 in GROUPS]
         ws = keep.tile([P, PACK, P], U8, name="ws", align_bytes=64)
         banks = [psum.tile([P, S], F32, name=f"bank{t}") for t in range(PACK)]
         for u, (t0, t1) in enumerate(GROUPS):
-            for cols in ((slice(0, P // 2), slice(P // 2, P)) if u == 0 else (slice(0, P),)):
-                nc.vector.quantize_mx(out=wq[u][:, :, cols].rearrange("p t m -> p (t m)").bitcast(FP8X4), scales=ws[:, t0:t1, cols].rearrange("p t m -> p (t m)"),
-                                      in_=wb[t0 // 2][:, t0 % 2 : t0 % 2 + t1 - t0, cols].rearrange("p t m j -> p (t m j)"))
+            for part in FIRST_TILE_PARTS if t0 == 0 else [slice(0, P)]:
+                nc.vector.quantize_mx(out=wq[u][:, :, part].rearrange("p t m -> p (t m)").bitcast(FP8X4),
+                                      scales=ws[:, t0:t1, part].rearrange("p t m -> p (t m)"),
+                                      in_=wb[t0 // 2][:, t0 % 2 : t0 % 2 + t1 - t0, part].rearrange("p t m j -> p (t m j)"))
             for t in range(t0, t1):
                 nc.tensor.matmul_mx(out=banks[t][:], lhsT=wq[u][:, t - t0, :].bitcast(FP8X4), lhsT_scale=ws[:, t, :],
                                     rhs=xw[:].bitcast(FP8X4), rhs_scale=xs[:], start=True, stop=True)
@@ -127,9 +130,9 @@ def tile_picked_rank_none_po_kernel(tc, x_words, x_scales, w1, offs, out_0, out_
             engine_copy(yb[h][:, a - HALF * h : b - HALF * h, :].rearrange("p (c i) t -> p c t i", i=2),
                         y[:, :, a:b].rearrange("p t (c i) -> p c t i", i=2))
 
-        weave(nc.vector.tensor_copy, 0, HALF)
-        weave(nc.scalar.copy, VECTOR_WEAVE, S)
-        weave(nc.vector.tensor_copy, HALF, VECTOR_WEAVE)
+        for h in range(2):
+            weave(nc.vector.tensor_copy, HALF * h, VECTOR_WEAVE[h])
+            weave(nc.scalar.copy, VECTOR_WEAVE[h], HALF * (h + 1))
 
         words_out = out_1[0].rearrange("p n t -> p (n t)").bitcast(I32)
         for h in range(2):

@@ -135,10 +135,11 @@ def tile_picked_rank_none_po_kernel(tc, x_words, x_scales, w1, offs, out_0, out_
             weave(nc.scalar.copy, VECTOR_WEAVE[h], HALF * (h + 1))
 
         words_out = out_1[0].rearrange("p n t -> p (n t)").bitcast(I32)
-        for h in range(2):
-            cols = slice(HALF * h, HALF * (h + 1))
+        halves = [slice(HALF * h, HALF * (h + 1)) for h in range(2)]
+        for h, cols in enumerate(halves):
             nc.vector.quantize_mx(out=yq[:, cols].bitcast(FP8X4), scales=ys[:, cols], in_=yb[h][:].rearrange("p c t -> p (c t)"))
-            nc.sync.dma_start(words_out[:, cols], yq[:, cols].bitcast(I32))
+        nc.sync.dma_start(words_out[:, halves[0]], yq[:, halves[0]].bitcast(I32))
         for r in range(PACK):
             queue = nc.scalar if r % 2 == 0 else nc.sync
             queue.dma_start(out_2[0][r:SCALE_ROWS:PACK, :].bitcast(I32), ys[r:P:QUADRANT, :].bitcast(I32))
+        nc.sync.dma_start(words_out[:, halves[1]], yq[:, halves[1]].bitcast(I32))

@@ -29,7 +29,7 @@ VECTOR_M = 56
 GROUPS = [(0, 1), (1, 2), (2, 4)]
 FIRST_TILE_PARTS = [slice(0, P // 2), slice(P // 2, P)]
 EARLY_COLUMNS = 384
-VECTOR_WEAVE = (176, 400)
+VECTOR_WEAVE = (176, 408)
 
 
 def tile_picked_rank_none_po_kernel(tc, x_words, x_scales, w1, offs, out_0, out_1, out_2):
@@ -113,10 +113,9 @@ def tile_picked_rank_none_po_kernel(tc, x_words, x_scales, w1, offs, out_0, out_
         invert(2)
         normalise_on_vector(1, slice(0, EARLY_COLUMNS))
         nc.sync.dma_start(out_rows[:, :first_store], y_rows[:, :first_store])
-        normalise_on_scalar(2, slice(0, HALF))
-        normalise_on_scalar(2, slice(HALF, S))
+        normalise_on_scalar(2, slice(0, S))
         invert(3)
-        normalise_on_vector(1, slice(EARLY_COLUMNS, S))
+        normalise_on_scalar(1, slice(EARLY_COLUMNS, S))
         normalise_on_vector(3, slice(0, HALF))
         normalise_on_vector(3, slice(HALF, S))
         nc.sync.dma_start(out_rows[:, first_store:], y_rows[:, first_store:])

@@ -139,6 +139,6 @@ def tile_picked_rank_none_po_kernel(tc, x_words, x_scales, w1, offs, out_0, out_
             nc.vector.quantize_mx(out=yq[:, cols].bitcast(FP8X4), scales=ys[:, cols], in_=yb[h][:].rearrange("p c t -> p (c t)"))
         nc.sync.dma_start(words_out[:, halves[0]], yq[:, halves[0]].bitcast(I32))
         for r in range(PACK):
-            queue = nc.scalar if r % 2 == 0 else nc.sync
+            queue = nc.sync if r == 0 else nc.scalar
             queue.dma_start(out_2[0][r:SCALE_ROWS:PACK, :].bitcast(I32), ys[r:P:QUADRANT, :].bitcast(I32))
         nc.sync.dma_start(words_out[:, halves[1]], yq[:, halves[1]].bitcast(I32))

@@ -29,7 +29,7 @@ VECTOR_M = 56
 GROUPS = [(0, 1), (1, 2), (2, 4)]
 FIRST_TILE_PARTS = [slice(0, P // 2), slice(P // 2, P)]
 EARLY_COLUMNS = 384
-VECTOR_WEAVE = (176, 408)
+VECTOR_WEAVE = (176, 392)
 
 
 def tile_picked_rank_none_po_kernel(tc, x_words, x_scales, w1, offs, out_0, out_1, out_2):

from contextlib import ExitStack

import concourse.mybir as mybir

K, T, S, N = 512, 1024, 512, 512
FLOPS = 2 * K * S * N
BYTES = 4 * K * N + K * S + K * S // 32 + 128 * S // 16 * 2 + 4 * N * S + N * S + N * S // 32

F32 = mybir.dt.float32
BF16 = mybir.dt.bfloat16
I32 = mybir.dt.int32
U32 = mybir.dt.uint32
U16 = mybir.dt.uint16
U8 = mybir.dt.uint8
FP8X4 = mybir.dt.float8_e4m3fn_x4
ACT = mybir.ActivationFunctionType
ALU = mybir.AluOpType
AX = mybir.AxisListType

P = 128
PACK = 4
QUADRANT = 32
SCALE_ROWS = 16
HALF = S // 2
EARLY_M = 96
SCALAR_M = 72
VECTOR_M = 56

GROUPS = [(0, 1), (1, 2), (2, 4)]
FIRST_TILE_PARTS = [slice(0, P // 2), slice(P // 2, P)]
EARLY_COLUMNS = 384
VECTOR_WEAVE = (176, 392)


def tile_picked_rank_none_po_kernel(tc, x_words, x_scales, w1, offs, out_0, out_1, out_2):
    nc = tc.nc
    with ExitStack() as ctx:
        keep = ctx.enter_context(tc.tile_pool(name="keep", bufs=1))
        psum = ctx.enter_context(tc.psum_pool(name="psum", bufs=1))

        offsets = keep.tile([P, S // 16], U16, name="offsets")

        xs_all = keep.tile([P, T], U8, name="xs_all", align_bytes=64)
        xw_all = keep.tile([P, T], U32, name="xw_all", align_bytes=64)
        w_rows = w1.rearrange("(p j) c -> p j c", j=PACK)
        w_lo = keep.tile([P, PACK, PACK * EARLY_M], F32, name="w_lo")
        w_hi = keep.tile([P, PACK, N - PACK * EARLY_M], F32, name="w_hi")
        nc.vector.memset(xs_all[:].bitcast(I32), 0)
        nc.sync.dma_start(xw_all[:].bitcast(I32), x_words[0].rearrange("p n t -> p (n t)").bitcast(I32))
        nc.sync.dma_start(offsets[:], offs)
        for r in range(PACK):
            nc.sync.dma_start(xs_all[r:P:QUADRANT, :].bitcast(I32), x_scales[0][r:SCALE_ROWS:PACK, :].bitcast(I32))
        nc.sync.dma_start(w_lo[:], w_rows[:, :, : PACK * EARLY_M])
        nc.sync.dma_start(w_hi[:], w_rows[:, :, PACK * EARLY_M :])

        xs = keep.tile([P, S], U8, name="xs", align_bytes=64)
        xw = keep.tile([P, S], U32, name="xw", align_bytes=64)
        nc.vector.tensor_copy(xw[:], xw_all[:].indirect(offsets[:]))
        nc.vector.tensor_copy(xs[:], xs_all[:].indirect(offsets[:]))

        wb = [keep.tile([P, 2, P, PACK], BF16, name=f"wb{pair}", tag=f"wb{pair}", align_bytes=64) for pair in range(2)]

        def deal(engine_copy, pair, m0, m1):
            src, first_m = (w_lo, 0) if m0 < EARLY_M else (w_hi, EARLY_M)
            engine_copy(wb[pair][:, :, m0:m1, :].rearrange("p t m j -> p m j t"),
                        src[:].rearrange("p j (m t) -> p m j t", t=PACK)[:, m0 - first_m : m1 - first_m, :, 2 * pair : 2 * pair + 2])

        deal(nc.scalar.copy, 0, 0, SCALAR_M)
        deal(nc.vector.tensor_copy, 0, SCALAR_M, EARLY_M)
        deal(nc.vector.tensor_copy, 1, 0, VECTOR_M)
        deal(nc.scalar.copy, 0, EARLY_M, P)
        deal(nc.scalar.copy, 1, VECTOR_M, EARLY_M)
        deal(nc.scalar.copy, 1, EARLY_M, P)

        wq = [keep.tile([P, t1 - t0, P], U32, name=f"wq{t0}", tag="wb0" if t0 == 2 else f"wq{t0}", align_bytes=64) for t0, t1 in GROUPS]
        ws = keep.tile([P, PACK, P], U8, name="ws", align_bytes=64)
        banks = [psum.tile([P, S], F32, name=f"bank{t}") for t in range(PACK)]
        for u, (t0, t1) in enumerate(GROUPS):
            for part in FIRST_TILE_PARTS if t0 == 0 else [slice(0, P)]:
                nc.vector.quantize_mx(out=wq[u][:, :, part].rearrange("p t m -> p (t m)").bitcast(FP8X4),
                                      scales=ws[:, t0:t1, part].rearrange("p t m -> p (t m)"),
                                      in_=wb[t0 // 2][:, t0 % 2 : t0 % 2 + t1 - t0, part].rearrange("p t m j -> p (t m j)"))
            for t in range(t0, t1):
                nc.tensor.matmul_mx(out=banks[t][:], lhsT=wq[u][:, t - t0, :].bitcast(FP8X4), lhsT_scale=ws[:, t, :],
                                    rhs=xw[:].bitcast(FP8X4), rhs_scale=xs[:], start=True, stop=True)

        neg_max = [keep.tile([P, 1], F32, name=f"neg_max{t}") for t in range(PACK)]
        total = keep.tile([P, PACK], F32, name="total")
        inv = keep.tile([P, PACK], F32, name="inv")
        e = [keep.tile([P, S], F32, name=f"e{t}") for t in range(PACK)]
        y = keep.tile([P, PACK, S], F32, name="y")
        out_rows = out_0.rearrange("(p t) c -> p (t c)", t=PACK)
        y_rows = y[:].rearrange("p t c -> p (t c)")

        def invert(t):
            nc.vector.reciprocal(inv[:, t : t + 1], total[:, t : t + 1])

        def normalise_on_vector(t, cols):
            nc.vector.tensor_scalar(y[:, t, cols], e[t][:, cols], inv[:, t : t + 1], None, ALU.mult)

        def normalise_on_scalar(t, cols):
            nc.scalar.activation(y[:, t, cols], e[t][:, cols], ACT.Copy, scale=inv[:, t : t + 1])

        for t in range(PACK):
            if t == PACK - 1:
                invert(0)
            nc.vector.tensor_reduce(neg_max[t][:], banks[t][:], AX.X, ALU.max, negate=True)
            nc.scalar.activation(e[t][:], banks[t][:], ACT.Exp, bias=neg_max[t][:], scale=1.0, accum_out=total[:, t : t + 1])

        first_store = S + EARLY_COLUMNS
        invert(1)
        normalise_on_vector(0, slice(0, S))
        invert(2)
        normalise_on_vector(1, slice(0, EARLY_COLUMNS))
        nc.sync.dma_start(out_rows[:, :first_store], y_rows[:, :first_store])
        normalise_on_scalar(2, slice(0, S))
        invert(3)
        normalise_on_scalar(1, slice(EARLY_COLUMNS, S))
        normalise_on_vector(3, slice(0, HALF))
        normalise_on_vector(3, slice(HALF, S))
        nc.sync.dma_start(out_rows[:, first_store:], y_rows[:, first_store:])

        yb = [keep.tile([P, HALF, PACK], BF16, name=f"yb{h}", align_bytes=64) for h in range(2)]
        yq = keep.tile([P, S], U32, name="yq", align_bytes=64)
        ys = keep.tile([P, S], U8, name="ys", align_bytes=64)

        def weave(engine_copy, a, b):
            h = a // HALF
            engine_copy(yb[h][:, a - HALF * h : b - HALF * h, :].rearrange("p (c i) t -> p c t i", i=2),
                        y[:, :, a:b].rearrange("p t (c i) -> p c t i", i=2))

        for h in range(2):
            weave(nc.vector.tensor_copy, HALF * h, VECTOR_WEAVE[h])
            weave(nc.scalar.copy, VECTOR_WEAVE[h], HALF * (h + 1))

        words_out = out_1[0].rearrange("p n t -> p (n t)").bitcast(I32)
        halves = [slice(HALF * h, HALF * (h + 1)) for h in range(2)]
        for h, cols in enumerate(halves):
            nc.vector.quantize_mx(out=yq[:, cols].bitcast(FP8X4), scales=ys[:, cols], in_=yb[h][:].rearrange("p c t -> p (c t)"))
        nc.sync.dma_start(words_out[:, halves[0]], yq[:, halves[0]].bitcast(I32))
        for r in range(PACK):
            queue = nc.sync if r == 0 else nc.scalar
            queue.dma_start(out_2[0][r:SCALE_ROWS:PACK, :].bitcast(I32), ys[r:P:QUADRANT, :].bitcast(I32))
        nc.sync.dma_start(words_out[:, halves[1]], yq[:, halves[1]].bitcast(I32))
